import numpy as np
import ml_dtypes


def mxq(x, axis, fmt="e4m3"):
    dtype, down = {"e4m3": (ml_dtypes.float8_e4m3fn, 7), "e5m2": (ml_dtypes.float8_e5m2, 14)}[fmt]
    v = np.moveaxis(np.asarray(x, np.float32).astype(ml_dtypes.bfloat16).astype(np.float64), axis, -1)
    blocks = v.reshape(v.shape[:-1] + (-1, 32))
    amax = np.abs(blocks).max(-1, keepdims=True)
    byte = np.maximum(np.where(amax > 0, np.frexp(amax)[1] - 1 + 127, 0) - down, 1)
    scale = np.exp2(byte - 127.0)
    codes = (blocks / scale).astype(np.float32).astype(dtype).astype(np.float64)
    return np.moveaxis((codes * scale).reshape(v.shape), -1, axis)


WIDE = False


def mx_kscale(k):
    if not WIDE:
        return np.ones(k)
    levels = np.array([10, -10, 5, -5, 0])
    if k % 512:
        return np.exp2(np.random.permutation(np.resize(levels, k // 32))).repeat(32)
    a = np.empty((k // 512, 16))
    for p in range(k // 512):
        a[p, :8] = np.random.permutation(np.resize(levels, 8))
        for g in range(8):
            far = levels[np.abs(levels - a[p, g]) >= 10]
            a[p, g + 8] = far[np.random.randint(len(far))]
    return np.exp2(a.ravel()).repeat(32)


def f64(x):
    return np.asarray(x).astype(np.float64)


def striped(idx):
    return np.tile(idx.reshape(-1, 16).T, (8, 1)).astype(np.uint16)


def unstriped(offs):
    return offs[:16].T.reshape(-1).astype(np.int64)


def gelu(v):
    return 0.5 * v * (1.0 + np.tanh(np.sqrt(2.0 / np.pi) * (v + 0.044715 * v**3)))


K, T, E, C, N = 2560, 768, 2, 256, 256


def by_expert(wq, xq):
    return np.concatenate([wq[e].T @ xq[:, e * C:(e + 1) * C] for e in range(E)], axis=1)


def setup_inputs():
    n = np.random.standard_normal
    s = mx_kscale(K)[:, None]
    return {
        "xT": (n((K, T)) * s).astype(np.float32),
        "w": (n((E + 1, K, N)) / np.sqrt(K) / s[None]).astype(np.float32),
        "b": (0.3 * n((N, E + 1))).astype(np.float32),
        "gate": np.tile(np.random.uniform(0.2, 1.0, E * C), (N, 1)).astype(np.float32),
        "offs": striped(np.random.permutation(T)[:E * C]),
    }


def reference(xT, w, b, gate, offs):
    idx = unstriped(offs)
    wq = mxq(f64(w), 1, "e4m3")
    xs = mxq(f64(xT), 0, "e4m3")
    ys = gelu((wq[E].T @ xs) + f64(b)[:, E:])
    xq = mxq(f64(xT)[:, idx], 0, "e4m3")
    y = by_expert(wq, xq)
    y = gelu(y + np.repeat(f64(b)[:, :E], C, axis=1))
    out = ys
    out[:, idx] += f64(gate) * y
    return out

@@ -1,0 +1,208 @@
+from contextlib import ExitStack
+
+import concourse.mybir as mybir
+
+K, T, E, C, N = 2560, 768, 2, 256, 256
+FLOPS = 2 * K * N * (E * C + T)
+
+F32 = mybir.dt.float32
+BF16 = mybir.dt.bfloat16
+U32 = mybir.dt.uint32
+I32 = mybir.dt.int32
+U16 = mybir.dt.uint16
+U8 = mybir.dt.uint8
+FP8X4 = mybir.dt.float8_e4m3fn_x4
+GELU = mybir.ActivationFunctionType.Gelu_apprx_tanh
+MULT = mybir.AluOpType.mult
+ADD = mybir.AluOpType.add
+
+P = 128
+PASSES = K // 512
+S = E * C
+W = T + S
+HALF = N // P
+XCUT = {(0,0): 384}
+GP = []
+VP = []
+
+
+def tile_moe_shr_lin_gelu_kernel(tc, xT, w, b, gate, offs, out):
+    nc = tc.nc
+    with ExitStack() as ctx:
+        held = ctx.enter_context(tc.tile_pool(name="held", bufs=1))
+        xraw = ctx.enter_context(tc.tile_pool(name="xraw", bufs=10))
+        wraw = ctx.enter_context(tc.tile_pool(name="wraw", bufs=8))
+        stage = ctx.enter_context(tc.tile_pool(name="stage", bufs=2))
+        psum = ctx.enter_context(tc.psum_pool(name="psum", bufs=1))
+
+        offsets = held.tile([P, S // 16], U16, name="offsets")
+        nc.sync.dma_start(offsets[:], offs)
+
+        bias = held.tile([P, HALF, E + 1], F32, name="bias")
+        gates = [held.tile([P, HALF, C], F32, name=f"gates{e}") for e in range(E)]
+        warm = held.tile([P, 1], F32, name="warm")
+        nc.vector.memset(warm[:], 0.0)
+        nc.scalar.activation(out=warm[:], in_=warm[:], func=GELU)
+
+        xcodes = [held.tile([P, W], U32, name=f"xcodes{c}", align_bytes=64) for c in range(PASSES)]
+        xscales = [held.tile([P, W], U8, name=f"xscales{c}", align_bytes=64) for c in range(PASSES)]
+        routed = [held.tile([P, T], F32, name=f"routed{m}") for m in range(HALF)]
+        for m in range(HALF):
+            nc.gpsimd.memset(routed[m][:], 0.0)
+        y = [[held.tile([P, C], F32, name=f"y{e}_{m}") for m in range(HALF)] for e in range(E)]
+        acc = [[psum.tile([P, 512], F32, name=f"acc{e}_{m}") for m in range(HALF)] for e in range(E)]
+        accs = [[psum.tile([P, 512], F32, name=f"accs{m}_{q}") for q in range(2)] for m in range(HALF)]
+        xr, wr = {}, {}
+
+        def load_x(c, h):
+            rows = xT[c * 512 : (c + 1) * 512, :].rearrange("(p h i) t -> p h i t", h=2, i=2)
+            t = xraw.tile([P, 2, T], F32, name="xrawt")
+            nc.sync.dma_start(out=t[:], in_=rows[:, h, :, :])
+            xr[c, h] = t
+
+        def load_w(e, c):
+            t = wraw.tile([P, 4, N], F32, name="wrawt")
+            nc.sync.dma_start(out=t[:], in_=w[e, c * 512 : (c + 1) * 512, :].rearrange("(p j) n -> p j n", j=4))
+            wr[e, c] = t
+
+        def load_gate(e):
+            nc.sync.dma_start(out=gates[e][:], in_=gate[:, e * C : (e + 1) * C].rearrange("(m p) s -> p m s", p=P))
+
+        def quant(c, xi):
+            flat = xi[:].rearrange("p t j -> p (t j)")
+            for a, z in ((0, 1024), (1024, 1280)):
+                nc.vector.quantize_mx(
+                    out=xcodes[c][:, a:z].bitcast(FP8X4), scales=xscales[c][:, a:z], in_=flat[:, 4 * a : 4 * z]
+                )
+
+        def tokens(c):
+            xg = stage.tile([P, 2, T, 2], BF16, name="xg", bufs=4, align_bytes=64)
+            xi = stage.tile([P, W, 4], BF16, name="xi", bufs=2, align_bytes=64)
+            words = xg[:].rearrange("p h t i -> p (h t i)")
+            iwords = xi[:].rearrange("p t j -> p (t j)")
+            for h in range(2):
+                cut = XCUT.get((c, h), T)
+                if cut > 0:
+                    nc.scalar.copy(out=xg[:, h, 0:cut, :], in_=xr[c, h][:, :, 0:cut].rearrange("p i t -> p t i"))
+                if cut < T:
+                    nc.vector.tensor_copy(
+                        out=xg[:, h, cut:T, :], in_=xr[c, h][:, :, cut:T].rearrange("p i t -> p t i")
+                    )
+                nc.vector.tensor_copy(
+                    iwords.bitcast(U32)[:, 2 * T + h : 2 * W : 2],
+                    words.bitcast(U32)[:, h * T : (h + 1) * T].indirect(offsets[:]),
+                )
+            nc.vector.tensor_copy(
+                out=iwords.bitcast(I32).rearrange("p (t h) -> p t h", h=2)[:, 0:T, :],
+                in_=words.bitcast(I32).rearrange("p (h t) -> p t h", h=2),
+            )
+            return c, xi
+
+        def scatter(e):
+            for m in range(HALF):
+                where = offsets[:, e * (C // 16) : (e + 1) * (C // 16)]
+                nc.vector.tensor_tensor(routed[m][:].indirect(where), y[e][m][:], gates[e][:, m, :], MULT)
+
+        def weights(gi, items):
+            n = len(items)
+            wi = stage.tile([P, 2, N, 4], BF16, name="wi", bufs=6, align_bytes=64)
+            wcodes = held.tile([P, n, N], U32, name=f"wcodes{gi}", align_bytes=64)
+            wscales = held.tile([P, n, N], U8, name=f"wscales{gi}", align_bytes=64)
+            for u, (e, c) in enumerate(items):
+                dst = wi[:, u].rearrange("p (c i) t -> p c t i", i=4)
+                src = wr[e, c][:].rearrange("p t (c i) -> p c t i", i=4)
+                if (e, c) in GP:
+                    nc.gpsimd.tensor_scalar(out=dst, in0=src, scalar1=1.0, scalar2=0.0, op0=MULT, op1=ADD)
+                elif (e, c) in VP:
+                    nc.vector.tensor_copy(out=dst, in_=src)
+                else:
+                    nc.scalar.copy(out=dst, in_=src)
+            nc.vector.quantize_mx(
+                out=wcodes[:].rearrange("p c n -> p (c n)").bitcast(FP8X4),
+                scales=wscales[:].rearrange("p c n -> p (c n)"),
+                in_=wi[:, 0:n].rearrange("p c n j -> p (c n j)"),
+            )
+            for u, (e, c) in enumerate(items):
+                begun[e] += 1
+                for m in range(HALF):
+                    cols = slice(m * P, (m + 1) * P)
+                    if e < E:
+                        parts = [(acc[e][m][:, 0:C], T + e * C, T + (e + 1) * C)]
+                    else:
+                        parts = [(accs[m][0][:, 0:512], 0, 512), (accs[m][1][:, 0:256], 512, 768)]
+                    for dst, a, z in parts:
+                        nc.tensor.matmul_mx(
+                            out=dst,
+                            lhsT=wcodes[:, u, cols].bitcast(FP8X4),
+                            lhsT_scale=wscales[:, u, cols],
+                            rhs=xcodes[c][:, a:z].bitcast(FP8X4),
+                            rhs_scale=xscales[c][:, a:z],
+                            start=(begun[e] == 1),
+                            stop=(begun[e] == PASSES),
+                        )
+                if begun[e] == PASSES and e < E:
+                    for m in range(HALF):
+                        nc.scalar.activation(out=y[e][m][:], in_=acc[e][m][:, 0:C], func=GELU, bias=bias[:, m, e : e + 1])
+
+        def finish():
+            for m in range(HALF):
+                for q, (a, z) in enumerate(((0, 512), (512, 768))):
+                    ys = stage.tile([P, 512], F32, name="ys", bufs=2)
+                    nc.scalar.activation(
+                        out=ys[:, 0 : z - a], in_=accs[m][q][:, 0 : z - a], func=GELU, bias=bias[:, m, E : E + 1]
+                    )
+                    res = stage.tile([P, 512], F32, name="res", bufs=2)
+                    nc.vector.tensor_tensor(res[:, 0 : z - a], ys[:, 0 : z - a], routed[m][:, a:z], ADD)
+                    nc.sync.dma_start(out=out[m * P : (m + 1) * P, a:z], in_=res[:, 0 : z - a])
+
+        begun = [0] * (E + 1)
+        load_x(0, 0)
+        load_x(0, 1)
+        load_x(1, 0)
+        load_w(2, 0)
+        load_x(1, 1)
+        load_x(2, 0)
+        load_x(2, 1)
+        load_x(3, 0)
+        load_x(3, 1)
+        load_x(4, 0)
+        load_w(0, 0)
+        load_w(1, 0)
+        load_w(2, 1)
+        load_w(0, 1)
+        load_w(1, 1)
+        load_w(2, 2)
+        load_gate(0)
+        load_w(0, 2)
+        load_x(4, 1)
+        load_w(1, 2)
+        load_w(0, 3)
+        load_w(1, 3)
+        load_w(0, 4)
+        nc.sync.dma_start(out=bias[:], in_=b.rearrange("(m p) e -> p m e", p=P))
+        load_w(1, 4)
+        load_w(2, 3)
+        load_w(2, 4)
+        load_gate(1)
+
+        last = None
+        for c in range(PASSES):
+            now = tokens(c)
+            if last is not None:
+                quant(*last)
+            last = now
+        quant(*last)
+
+        weights(0, ((2, 0),))
+        weights(1, ((0, 0),))
+        weights(2, ((1, 0), (2, 1),))
+        weights(3, ((0, 1), (1, 1),))
+        weights(4, ((2, 2), (0, 2),))
+        weights(5, ((1, 2),))
+        weights(6, ((0, 3),))
+        weights(7, ((1, 3), (0, 4),))
+        weights(8, ((1, 4),))
+        weights(9, ((2, 3), (2, 4),))
+        scatter(0)
+        scatter(1)
+        finish()

@@ -23,7 +23,7 @@ W = T + S
 HALF = N // P
 XCUT = {(0,0): 384}
 GP = []
-VP = []
+VP = [(0, 3)]
 
 
 def tile_moe_shr_lin_gelu_kernel(tc, xT, w, b, gate, offs, out):
@@ -78,6 +78,8 @@ def tile_moe_shr_lin_gelu_kernel(tc, xT, w, b, gate, offs, out):
         def tokens(c):
             xg = stage.tile([P, 2, T, 2], BF16, name="xg", bufs=4, align_bytes=64)
             xi = stage.tile([P, W, 4], BF16, name="xi", bufs=2, align_bytes=64)
+            gx = stage.tile([P, 2, S, 2], BF16, name="gx", align_bytes=64)
+            picked = gx[:].rearrange("p h s i -> p (h s i)")
             words = xg[:].rearrange("p h t i -> p (h t i)")
             iwords = xi[:].rearrange("p t j -> p (t j)")
             for h in range(2):
@@ -89,13 +91,14 @@ def tile_moe_shr_lin_gelu_kernel(tc, xT, w, b, gate, offs, out):
                         out=xg[:, h, cut:T, :], in_=xr[c, h][:, :, cut:T].rearrange("p i t -> p t i")
                     )
                 nc.vector.tensor_copy(
-                    iwords.bitcast(U32)[:, 2 * T + h : 2 * W : 2],
+                    picked.bitcast(U32)[:, h * S : (h + 1) * S],
                     words.bitcast(U32)[:, h * T : (h + 1) * T].indirect(offsets[:]),
                 )
-            nc.vector.tensor_copy(
-                out=iwords.bitcast(I32).rearrange("p (t h) -> p t h", h=2)[:, 0:T, :],
-                in_=words.bitcast(I32).rearrange("p (h t) -> p t h", h=2),
-            )
+            for a, z, src in ((0, T, words), (T, W, picked)):
+                nc.vector.tensor_copy(
+                    out=iwords.bitcast(I32).rearrange("p (t h) -> p t h", h=2)[:, a:z, :],
+                    in_=src.bitcast(I32).rearrange("p (h t) -> p t h", h=2),
+                )
             return c, xi
 
         def scatter(e):
@@ -105,7 +108,7 @@ def tile_moe_shr_lin_gelu_kernel(tc, xT, w, b, gate, offs, out):
 
         def weights(gi, items):
             n = len(items)
-            wi = stage.tile([P, 2, N, 4], BF16, name="wi", bufs=6, align_bytes=64)
+            wi = stage.tile([P, 2, N, 4], BF16, name="wi", bufs=5, align_bytes=64)
             wcodes = held.tile([P, n, N], U32, name=f"wcodes{gi}", align_bytes=64)
             wscales = held.tile([P, n, N], U8, name=f"wscales{gi}", align_bytes=64)
             for u, (e, c) in enumerate(items):
@@ -147,43 +150,42 @@ def tile_moe_shr_lin_gelu_kernel(tc, xT, w, b, gate, offs, out):
         def finish():
             for m in range(HALF):
                 for q, (a, z) in enumerate(((0, 512), (512, 768))):
-                    ys = stage.tile([P, 512], F32, name="ys", bufs=2)
+                    ys = stage.tile([P, 512], F32, name="ys", bufs=4)
                     nc.scalar.activation(
                         out=ys[:, 0 : z - a], in_=accs[m][q][:, 0 : z - a], func=GELU, bias=bias[:, m, E : E + 1]
                     )
-                    res = stage.tile([P, 512], F32, name="res", bufs=2)
-                    nc.vector.tensor_tensor(res[:, 0 : z - a], ys[:, 0 : z - a], routed[m][:, a:z], ADD)
-                    nc.sync.dma_start(out=out[m * P : (m + 1) * P, a:z], in_=res[:, 0 : z - a])
+                    nc.vector.tensor_tensor(ys[:, 0 : z - a], ys[:, 0 : z - a], routed[m][:, a:z], ADD)
+                    nc.sync.dma_start(out=out[m * P : (m + 1) * P, a:z], in_=ys[:, 0 : z - a])
 
         begun = [0] * (E + 1)
         load_x(0, 0)
         load_x(0, 1)
-        load_x(1, 0)
         load_w(2, 0)
+        load_x(1, 0)
         load_x(1, 1)
+        load_w(2, 1)
+        load_w(2, 2)
         load_x(2, 0)
         load_x(2, 1)
+        load_w(1, 0)
         load_x(3, 0)
         load_x(3, 1)
-        load_x(4, 0)
         load_w(0, 0)
-        load_w(1, 0)
-        load_w(2, 1)
+        load_x(4, 0)
         load_w(0, 1)
-        load_w(1, 1)
-        load_w(2, 2)
         load_gate(0)
-        load_w(0, 2)
-        load_x(4, 1)
-        load_w(1, 2)
-        load_w(0, 3)
-        load_w(1, 3)
-        load_w(0, 4)
-        nc.sync.dma_start(out=bias[:], in_=b.rearrange("(m p) e -> p m e", p=P))
-        load_w(1, 4)
+        load_w(1, 1)
         load_w(2, 3)
-        load_w(2, 4)
+        load_x(4, 1)
+        load_w(0, 2)
         load_gate(1)
+        nc.sync.dma_start(out=bias[:], in_=b.rearrange("(m p) e -> p m e", p=P))
+        load_w(1, 2)
+        load_w(1, 3)
+        load_w(0, 3)
+        load_w(2, 4)
+        load_w(0, 4)
+        load_w(1, 4)
 
         last = None
         for c in range(PASSES):
@@ -194,15 +196,15 @@ def tile_moe_shr_lin_gelu_kernel(tc, xT, w, b, gate, offs, out):
         quant(*last)
 
         weights(0, ((2, 0),))
-        weights(1, ((0, 0),))
-        weights(2, ((1, 0), (2, 1),))
-        weights(3, ((0, 1), (1, 1),))
-        weights(4, ((2, 2), (0, 2),))
-        weights(5, ((1, 2),))
-        weights(6, ((0, 3),))
-        weights(7, ((1, 3), (0, 4),))
-        weights(8, ((1, 4),))
-        weights(9, ((2, 3), (2, 4),))
+        weights(1, ((2, 1), (1, 0),))
+        weights(2, ((0, 0), (2, 2),))
+        weights(3, ((1, 1),))
+        weights(4, ((0, 1), (2, 3),))
+        weights(5, ((0, 2),))
+        weights(6, ((1, 2), (1, 3),))
+        weights(7, ((0, 3),))
+        weights(8, ((0, 4), (2, 4),))
+        weights(9, ((1, 4),))
         scatter(0)
         scatter(1)
         finish()

@@ -21,9 +21,9 @@ PASSES = K // 512
 S = E * C
 W = T + S
 HALF = N // P
-XCUT = {(0,0): 384}
+XCUT = {(0,1): 384, (0,0): 384, (4,0): 576, (3,0): 512}
 GP = []
-VP = [(0, 3)]
+VP = [(1, 4)]
 
 
 def tile_moe_shr_lin_gelu_kernel(tc, xT, w, b, gate, offs, out):
@@ -160,32 +160,32 @@ def tile_moe_shr_lin_gelu_kernel(tc, xT, w, b, gate, offs, out):
         begun = [0] * (E + 1)
         load_x(0, 0)
         load_x(0, 1)
-        load_w(2, 0)
+        load_w(1, 0)
         load_x(1, 0)
         load_x(1, 1)
-        load_w(2, 1)
-        load_w(2, 2)
+        load_w(1, 1)
         load_x(2, 0)
         load_x(2, 1)
-        load_w(1, 0)
         load_x(3, 0)
-        load_x(3, 1)
         load_w(0, 0)
+        load_w(2, 0)
+        load_w(2, 1)
+        load_x(3, 1)
         load_x(4, 0)
         load_w(0, 1)
-        load_gate(0)
-        load_w(1, 1)
-        load_w(2, 3)
-        load_x(4, 1)
         load_w(0, 2)
-        load_gate(1)
+        load_w(2, 2)
+        load_x(4, 1)
+        load_w(2, 3)
+        load_w(0, 3)
         nc.sync.dma_start(out=bias[:], in_=b.rearrange("(m p) e -> p m e", p=P))
+        load_w(0, 4)
         load_w(1, 2)
         load_w(1, 3)
-        load_w(0, 3)
-        load_w(2, 4)
-        load_w(0, 4)
         load_w(1, 4)
+        load_w(2, 4)
+        load_gate(0)
+        load_gate(1)
 
         last = None
         for c in range(PASSES):
@@ -195,16 +195,16 @@ def tile_moe_shr_lin_gelu_kernel(tc, xT, w, b, gate, offs, out):
             last = now
         quant(*last)
 
-        weights(0, ((2, 0),))
-        weights(1, ((2, 1), (1, 0),))
-        weights(2, ((0, 0), (2, 2),))
-        weights(3, ((1, 1),))
-        weights(4, ((0, 1), (2, 3),))
-        weights(5, ((0, 2),))
-        weights(6, ((1, 2), (1, 3),))
-        weights(7, ((0, 3),))
-        weights(8, ((0, 4), (2, 4),))
-        weights(9, ((1, 4),))
+        weights(0, ((1, 0),))
+        weights(1, ((1, 1),))
+        weights(2, ((0, 0), (2, 0),))
+        weights(3, ((0, 1), (2, 1),))
+        weights(4, ((0, 2), (2, 2),))
+        weights(5, ((2, 3),))
+        weights(6, ((0, 4),))
+        weights(7, ((0, 3), (1, 2),))
+        weights(8, ((1, 3), (1, 4),))
+        weights(9, ((2, 4),))
         scatter(0)
         scatter(1)
         finish()

from contextlib import ExitStack

import concourse.mybir as mybir

K, T, E, C, N = 2560, 768, 2, 256, 256
FLOPS = 2 * K * N * (E * C + T)

F32 = mybir.dt.float32
BF16 = mybir.dt.bfloat16
U32 = mybir.dt.uint32
I32 = mybir.dt.int32
U16 = mybir.dt.uint16
U8 = mybir.dt.uint8
FP8X4 = mybir.dt.float8_e4m3fn_x4
GELU = mybir.ActivationFunctionType.Gelu_apprx_tanh
MULT = mybir.AluOpType.mult
ADD = mybir.AluOpType.add

P = 128
PASSES = K // 512
S = E * C
W = T + S
HALF = N // P
XCUT = {(0,1): 384, (0,0): 384, (4,0): 576, (3,0): 512}
GP = []
VP = [(1, 4)]


def tile_moe_shr_lin_gelu_kernel(tc, xT, w, b, gate, offs, out):
    nc = tc.nc
    with ExitStack() as ctx:
        held = ctx.enter_context(tc.tile_pool(name="held", bufs=1))
        xraw = ctx.enter_context(tc.tile_pool(name="xraw", bufs=10))
        wraw = ctx.enter_context(tc.tile_pool(name="wraw", bufs=8))
        stage = ctx.enter_context(tc.tile_pool(name="stage", bufs=2))
        psum = ctx.enter_context(tc.psum_pool(name="psum", bufs=1))

        offsets = held.tile([P, S // 16], U16, name="offsets")
        nc.sync.dma_start(offsets[:], offs)

        bias = held.tile([P, HALF, E + 1], F32, name="bias")
        gates = [held.tile([P, HALF, C], F32, name=f"gates{e}") for e in range(E)]
        warm = held.tile([P, 1], F32, name="warm")
        nc.vector.memset(warm[:], 0.0)
        nc.scalar.activation(out=warm[:], in_=warm[:], func=GELU)

        xcodes = [held.tile([P, W], U32, name=f"xcodes{c}", align_bytes=64) for c in range(PASSES)]
        xscales = [held.tile([P, W], U8, name=f"xscales{c}", align_bytes=64) for c in range(PASSES)]
        routed = [held.tile([P, T], F32, name=f"routed{m}") for m in range(HALF)]
        for m in range(HALF):
            nc.gpsimd.memset(routed[m][:], 0.0)
        y = [[held.tile([P, C], F32, name=f"y{e}_{m}") for m in range(HALF)] for e in range(E)]
        acc = [[psum.tile([P, 512], F32, name=f"acc{e}_{m}") for m in range(HALF)] for e in range(E)]
        accs = [[psum.tile([P, 512], F32, name=f"accs{m}_{q}") for q in range(2)] for m in range(HALF)]
        xr, wr = {}, {}

        def load_x(c, h):
            rows = xT[c * 512 : (c + 1) * 512, :].rearrange("(p h i) t -> p h i t", h=2, i=2)
            t = xraw.tile([P, 2, T], F32, name="xrawt")
            nc.sync.dma_start(out=t[:], in_=rows[:, h, :, :])
            xr[c, h] = t

        def load_w(e, c):
            t = wraw.tile([P, 4, N], F32, name="wrawt")
            nc.sync.dma_start(out=t[:], in_=w[e, c * 512 : (c + 1) * 512, :].rearrange("(p j) n -> p j n", j=4))
            wr[e, c] = t

        def load_gate(e):
            nc.sync.dma_start(out=gates[e][:], in_=gate[:, e * C : (e + 1) * C].rearrange("(m p) s -> p m s", p=P))

        def quant(c, xi):
            flat = xi[:].rearrange("p t j -> p (t j)")
            for a, z in ((0, 1024), (1024, 1280)):
                nc.vector.quantize_mx(
                    out=xcodes[c][:, a:z].bitcast(FP8X4), scales=xscales[c][:, a:z], in_=flat[:, 4 * a : 4 * z]
                )

        def tokens(c):
            xg = stage.tile([P, 2, T, 2], BF16, name="xg", bufs=4, align_bytes=64)
            xi = stage.tile([P, W, 4], BF16, name="xi", bufs=2, align_bytes=64)
            gx = stage.tile([P, 2, S, 2], BF16, name="gx", align_bytes=64)
            picked = gx[:].rearrange("p h s i -> p (h s i)")
            words = xg[:].rearrange("p h t i -> p (h t i)")
            iwords = xi[:].rearrange("p t j -> p (t j)")
            for h in range(2):
                cut = XCUT.get((c, h), T)
                if cut > 0:
                    nc.scalar.copy(out=xg[:, h, 0:cut, :], in_=xr[c, h][:, :, 0:cut].rearrange("p i t -> p t i"))
                if cut < T:
                    nc.vector.tensor_copy(
                        out=xg[:, h, cut:T, :], in_=xr[c, h][:, :, cut:T].rearrange("p i t -> p t i")
                    )
                nc.vector.tensor_copy(
                    picked.bitcast(U32)[:, h * S : (h + 1) * S],
                    words.bitcast(U32)[:, h * T : (h + 1) * T].indirect(offsets[:]),
                )
            for a, z, src in ((0, T, words), (T, W, picked)):
                nc.vector.tensor_copy(
                    out=iwords.bitcast(I32).rearrange("p (t h) -> p t h", h=2)[:, a:z, :],
                    in_=src.bitcast(I32).rearrange("p (h t) -> p t h", h=2),
                )
            return c, xi

        def scatter(e):
            for m in range(HALF):
                where = offsets[:, e * (C // 16) : (e + 1) * (C // 16)]
                nc.vector.tensor_tensor(routed[m][:].indirect(where), y[e][m][:], gates[e][:, m, :], MULT)

        def weights(gi, items):
            n = len(items)
            wi = stage.tile([P, 2, N, 4], BF16, name="wi", bufs=5, align_bytes=64)
            wcodes = held.tile([P, n, N], U32, name=f"wcodes{gi}", align_bytes=64)
            wscales = held.tile([P, n, N], U8, name=f"wscales{gi}", align_bytes=64)
            for u, (e, c) in enumerate(items):
                dst = wi[:, u].rearrange("p (c i) t -> p c t i", i=4)
                src = wr[e, c][:].rearrange("p t (c i) -> p c t i", i=4)
                if (e, c) in GP:
                    nc.gpsimd.tensor_scalar(out=dst, in0=src, scalar1=1.0, scalar2=0.0, op0=MULT, op1=ADD)
                elif (e, c) in VP:
                    nc.vector.tensor_copy(out=dst, in_=src)
                else:
                    nc.scalar.copy(out=dst, in_=src)
            nc.vector.quantize_mx(
                out=wcodes[:].rearrange("p c n -> p (c n)").bitcast(FP8X4),
                scales=wscales[:].rearrange("p c n -> p (c n)"),
                in_=wi[:, 0:n].rearrange("p c n j -> p (c n j)"),
            )
            for u, (e, c) in enumerate(items):
                begun[e] += 1
                for m in range(HALF):
                    cols = slice(m * P, (m + 1) * P)
                    if e < E:
                        parts = [(acc[e][m][:, 0:C], T + e * C, T + (e + 1) * C)]
                    else:
                        parts = [(accs[m][0][:, 0:512], 0, 512), (accs[m][1][:, 0:256], 512, 768)]
                    for dst, a, z in parts:
                        nc.tensor.matmul_mx(
                            out=dst,
                            lhsT=wcodes[:, u, cols].bitcast(FP8X4),
                            lhsT_scale=wscales[:, u, cols],
                            rhs=xcodes[c][:, a:z].bitcast(FP8X4),
                            rhs_scale=xscales[c][:, a:z],
                            start=(begun[e] == 1),
                            stop=(begun[e] == PASSES),
                        )
                if begun[e] == PASSES and e < E:
                    for m in range(HALF):
                        nc.scalar.activation(out=y[e][m][:], in_=acc[e][m][:, 0:C], func=GELU, bias=bias[:, m, e : e + 1])

        def finish():
            for m in range(HALF):
                for q, (a, z) in enumerate(((0, 512), (512, 768))):
                    ys = stage.tile([P, 512], F32, name="ys", bufs=4)
                    nc.scalar.activation(
                        out=ys[:, 0 : z - a], in_=accs[m][q][:, 0 : z - a], func=GELU, bias=bias[:, m, E : E + 1]
                    )
                    nc.vector.tensor_tensor(ys[:, 0 : z - a], ys[:, 0 : z - a], routed[m][:, a:z], ADD)
                    nc.sync.dma_start(out=out[m * P : (m + 1) * P, a:z], in_=ys[:, 0 : z - a])

        begun = [0] * (E + 1)
        load_x(0, 0)
        load_x(0, 1)
        load_w(1, 0)
        load_x(1, 0)
        load_x(1, 1)
        load_w(1, 1)
        load_x(2, 0)
        load_x(2, 1)
        load_x(3, 0)
        load_w(0, 0)
        load_w(2, 0)
        load_w(2, 1)
        load_x(3, 1)
        load_x(4, 0)
        load_w(0, 1)
        load_w(0, 2)
        load_w(2, 2)
        load_x(4, 1)
        load_w(2, 3)
        load_w(0, 3)
        nc.sync.dma_start(out=bias[:], in_=b.rearrange("(m p) e -> p m e", p=P))
        load_w(0, 4)
        load_w(1, 2)
        load_w(1, 3)
        load_w(1, 4)
        load_w(2, 4)
        load_gate(0)
        load_gate(1)

        last = None
        for c in range(PASSES):
            now = tokens(c)
            if last is not None:
                quant(*last)
            last = now
        quant(*last)

        weights(0, ((1, 0),))
        weights(1, ((1, 1),))
        weights(2, ((0, 0), (2, 0),))
        weights(3, ((0, 1), (2, 1),))
        weights(4, ((0, 2), (2, 2),))
        weights(5, ((2, 3),))
        weights(6, ((0, 4),))
        weights(7, ((0, 3), (1, 2),))
        weights(8, ((1, 3), (1, 4),))
        weights(9, ((2, 4),))
        scatter(0)
        scatter(1)
        finish()
